import numpy as np
import ml_dtypes


def mxq(x, axis, fmt="e4m3"):
    dtype, down = {"e4m3": (ml_dtypes.float8_e4m3fn, 7), "e5m2": (ml_dtypes.float8_e5m2, 14)}[fmt]
    v = np.moveaxis(np.asarray(x, np.float32).astype(ml_dtypes.bfloat16).astype(np.float64), axis, -1)
    blocks = v.reshape(v.shape[:-1] + (-1, 32))
    amax = np.abs(blocks).max(-1, keepdims=True)
    byte = np.maximum(np.where(amax > 0, np.frexp(amax)[1] - 1 + 127, 0) - down, 1)
    scale = np.exp2(byte - 127.0)
    codes = (blocks / scale).astype(np.float32).astype(dtype).astype(np.float64)
    return np.moveaxis((codes * scale).reshape(v.shape), -1, axis)


WIDE = False


def mx_kscale(k):
    if not WIDE:
        return np.ones(k)
    levels = np.array([10, -10, 5, -5, 0])
    if k % 512:
        return np.exp2(np.random.permutation(np.resize(levels, k // 32))).repeat(32)
    a = np.empty((k // 512, 16))
    for p in range(k // 512):
        a[p, :8] = np.random.permutation(np.resize(levels, 8))
        for g in range(8):
            far = levels[np.abs(levels - a[p, g]) >= 10]
            a[p, g + 8] = far[np.random.randint(len(far))]
    return np.exp2(a.ravel()).repeat(32)


def f64(x):
    return np.asarray(x).astype(np.float64)


def striped(idx):
    return np.tile(idx.reshape(-1, 16).T, (8, 1)).astype(np.uint16)


def unstriped(offs):
    return offs[:16].T.reshape(-1).astype(np.int64)


def striped8(idx):
    return np.concatenate([x.reshape(-1, 16).T for x in idx]).astype(np.uint16)


def runs(offs, k):
    lists = np.stack([offs[16 * r : 16 * r + 16].T.reshape(-1) for r in range(8)]).astype(np.int64)
    return lists[np.arange(k) % 512 // 64]


def pack_weight(w):
    k, n = w.shape
    w = f64(np.asarray(w, np.float32).astype(ml_dtypes.bfloat16)).reshape(k // 32, 32, n)
    amax = np.abs(w).max(1)
    byte = np.clip(np.where(amax > 0, np.frexp(amax)[1] - 1 + 127 - 7, 1), 1, 254)
    scaled = (w * np.exp2(127.0 - byte)[:, None, :]).reshape(k, n).astype(np.float32)
    words = np.ascontiguousarray(scaled.reshape(k // 512, 128, 4, n).transpose(0, 1, 3, 2)).astype(ml_dtypes.float8_e4m3fn).view(np.uint8)
    return words, np.ascontiguousarray(byte.astype(np.uint8).reshape(k // 512, 16, n))


def unpack_weight(words, scales):
    g, p, n, _ = words.shape
    vals = np.ascontiguousarray(words).view(ml_dtypes.float8_e4m3fn).astype(np.float64) * np.repeat(np.exp2(scales.astype(np.float64) - 127.0), 8, axis=1)[..., None]
    return vals.transpose(0, 1, 3, 2).reshape(g * 512, n)


K, T, S, N, G, H, U = 512, 1024, 256, 512, 2048, 512, 512


def setup_inputs():
    n = np.random.standard_normal
    s = mx_kscale(K)[:, None]
    u = mx_kscale(K)
    packed_xT = pack_weight(n((K, T)) * s)
    packed_dT = pack_weight(n((K, G)) / s)
    perm = np.random.permutation(U)
    return {
        "x_words": packed_xT[0],
        "x_scales": packed_xT[1],
        "d_words": packed_dT[0],
        "d_scales": packed_dT[1],
        "gn": (np.random.uniform(0.5, 1.5, (H, 1)) * u[:, None]).astype(np.float32),
        "w1": (n((H, N)) / np.sqrt(H) / u[:, None]).astype(np.float32),
        "offs": striped8(np.random.randint(0, T, (8, S))),
        "ka": striped8(np.random.randint(0, G, (8, H))),
        "kb": striped8(np.random.randint(0, G, (8, H))),
        "n1": striped(perm[:S]),
        "n2": striped(perm[S:]),
        "n3": striped(np.random.permutation(S)),
    }


def reference(x_words, x_scales, d_words, d_scales, gn, w1, offs, ka, kb, n1, n2, n3):
    d_ka = unpack_weight(d_words, d_scales)[np.arange(K)[:, None], runs(ka, K)]
    xq = unpack_weight(x_words, x_scales)[np.arange(K)[:, None], runs(offs, K)]
    d_kb = unpack_weight(d_words, d_scales)[np.arange(K)[:, None], runs(kb, K)]
    h = 0.0625 * (d_ka.T @ xq + d_kb.T @ xq)
    z = f64(gn) * h
    h2 = mxq(f64(w1), 0, "e4m3").T @ mxq(z, 0, "e4m3")
    dn = np.minimum(h2, h2[:, unstriped(n3)])
    up = np.maximum(h2, h2[:, unstriped(n3)])
    ph = np.zeros((N, U))
    ph[:, unstriped(n1)] = up
    out = ph.copy()
    out[:, unstriped(n2)] = dn
    return out

@@ -1,0 +1,183 @@
+import concourse.mybir as mybir
+
+K, T, S, N, G, H, U = 512, 1024, 256, 512, 2048, 512, 512
+FLOPS = 2 * (2 * K * H * S + H * N * S)
+
+F32 = mybir.dt.float32
+BF16 = mybir.dt.bfloat16
+I32 = mybir.dt.int32
+U32 = mybir.dt.uint32
+U16 = mybir.dt.uint16
+U8 = mybir.dt.uint8
+FP8X4 = mybir.dt.float8_e4m3fn_x4
+ALU = mybir.AluOpType
+COPY = mybir.ActivationFunctionType.Copy
+
+P = 128
+PACK = 4
+RUN = 8
+HALF = S // 2
+SPARE = 16
+
+
+def tile_picked_haqipagmx_none_p_kernel(
+    tc, x_words, x_scales, d_words, d_scales, gn, w1, offs, ka, kb, n1, n2, n3, out
+):
+    nc = tc.nc
+    with (
+        tc.tile_pool(name="lists", bufs=1) as lists,
+        tc.tile_pool(name="sb", bufs=1) as sb,
+        tc.psum_pool(name="ps", bufs=1) as ps,
+    ):
+
+        def load_list(src, name):
+            tile = lists.tile(list(src.shape), U16, name=name)
+            nc.sync.dma_start(tile[:], src)
+            return tile
+
+        d_bytes = sb.tile([P, G], U8, align_bytes=64)
+        x_bytes = sb.tile([P, T], U8, align_bytes=64)
+        ka_t = load_list(ka, "ka_t")
+        nc.sync.dma_start(
+            d_bytes[:].bitcast(I32), d_scales[0].bitcast(I32).unsqueeze(1).to_broadcast([P // RUN, RUN, G // 4])
+        )
+        kb_t = load_list(kb, "kb_t")
+        offs_t = load_list(offs, "offs_t")
+        nc.sync.dma_start(
+            x_bytes[:].bitcast(I32), x_scales[0].bitcast(I32).unsqueeze(1).to_broadcast([P // RUN, RUN, T // 4])
+        )
+
+        x_table = sb.tile([P, T], U32, align_bytes=64)
+        d_table = sb.tile([P, G], U32, align_bytes=64)
+        nc.sync.dma_start(x_table[:].bitcast(I32), x_words[0].rearrange("p c t -> p (c t)").bitcast(I32))
+        nc.sync.dma_start(d_table[:].bitcast(I32), d_words[0].rearrange("p c t -> p (c t)").bitcast(I32))
+        n3_t = load_list(n3, "n3_t")
+        n1_t = load_list(n1, "n1_t")
+        n2_t = load_list(n2, "n2_t")
+
+        gain = sb.tile([P, PACK, 8], F32)
+        with nc.allow_non_contiguous_dma(reason="one gain for each partition and byte of a word"):
+            gn_view = gn.rearrange("(q t r) o -> t q r o", t=PACK, r=RUN)
+            for t in range(PACK):
+                nc.sync.dma_start(gain[:, t, 0:1], gn_view[t])
+
+        scales = sb.tile([P, 2 * H + S], U8, align_bytes=64)
+        nc.vector.memset(scales[:].bitcast(I32), 0)
+        rows = []
+        for b in range(N // P):
+            row = sb.tile([P, S + SPARE], F32, name="row%d" % b)
+            nc.gpsimd.memset(row[:, S:], 0.0)
+            rows.append(row)
+
+        picked_bytes = sb.tile([P, 2 * H + S], U8, tag="staging", align_bytes=64)
+        nc.vector.tensor_copy(picked_bytes[:, 0:H], d_bytes[:].indirect(ka_t[:]))
+        nc.vector.tensor_copy(picked_bytes[:, H : 2 * H], d_bytes[:].indirect(kb_t[:]))
+        nc.vector.tensor_copy(picked_bytes[:, 2 * H :], x_bytes[:].indirect(offs_t[:]))
+        dealt_bytes = sb.tile([P, 2 * H + S], U8, align_bytes=64)
+        nc.vector.tensor_copy(
+            dealt_bytes[:, : 2 * H].bitcast(I32).rearrange("p (l t q w) -> p l t q w", l=2, t=PACK, w=2),
+            picked_bytes[:, : 2 * H].bitcast(I32).rearrange("p (l q t w) -> p l t q w", l=2, t=PACK, w=2),
+        )
+        nc.vector.tensor_copy(dealt_bytes[:, 2 * H :].bitcast(I32), picked_bytes[:, 2 * H :].bitcast(I32))
+        for c in range(4):
+            queue = nc.sync if c % 2 == 0 else nc.scalar
+            queue.dma_start(scales[c:P:32, :].bitcast(I32), dealt_bytes[RUN * c : P : 32, :].bitcast(I32))
+
+        w_raw = sb.tile([P, PACK, N], F32, tag="staging", align_bytes=64)
+        w_view = w1.rearrange("(q t r) n -> t q r n", t=PACK, r=RUN)
+        for t in range(PACK):
+            nc.sync.dma_start(w_raw[:, t, :], w_view[t])
+
+        x_codes = sb.tile([P, S], U32, align_bytes=64)
+        nc.vector.tensor_copy(x_codes[:], x_table[:].indirect(offs_t[:]))
+        d_codes = []
+        for name, index in (("a", ka_t), ("b", kb_t)):
+            picked = sb.tile([P, H], U32, name="picked_" + name, align_bytes=64)
+            nc.vector.tensor_copy(picked[:], d_table[:].indirect(index[:]))
+            dealt = sb.tile([P, H], U32, name="dealt_" + name, align_bytes=64)
+            nc.vector.tensor_copy(
+                dealt[:].bitcast(I32).rearrange("p (t q r) -> p t q r", t=PACK, r=RUN),
+                picked[:].bitcast(I32).rearrange("p (q t r) -> p t q r", t=PACK, r=RUN),
+            )
+            d_codes.append(dealt)
+
+        h_banks = [ps.tile([P, PACK, HALF], F32, name="h%d" % u) for u in range(2)]
+        for l in range(2):
+            for u in range(2):
+                cols = slice(u * HALF, (u + 1) * HALF)
+                for t in range(PACK):
+                    nc.tensor.matmul_mx(
+                        out=h_banks[u][:, t, :],
+                        lhsT=d_codes[l][:, t * P : (t + 1) * P].bitcast(FP8X4),
+                        lhsT_scale=scales[:, l * H + t * P : l * H + (t + 1) * P],
+                        rhs=x_codes[:, cols].bitcast(FP8X4),
+                        rhs_scale=scales[:, 2 * H + u * HALF : 2 * H + (u + 1) * HALF],
+                        start=(l == 0 and t == 0),
+                        stop=(l == 1 and t == PACK - 1),
+                    )
+
+        w_codes = sb.tile([P, N], U32, align_bytes=64)
+        w_scales = sb.tile([P, N], U8, align_bytes=64)
+        for b in range(N // P):
+            cols = slice(b * P, (b + 1) * P)
+            w_bf = sb.tile([P, P, PACK], BF16, name="w_bf%d" % b, align_bytes=64)
+            nc.scalar.activation(
+                w_bf[:].rearrange("p (c i) t -> p c t i", i=4),
+                w_raw[:, :, cols].rearrange("p t (c i) -> p c t i", i=4),
+                COPY,
+            )
+            nc.vector.quantize_mx(
+                out=w_codes[:, cols].bitcast(FP8X4),
+                scales=w_scales[:, cols],
+                in_=w_bf[:].rearrange("p m t -> p (m t)"),
+            )
+
+        z_codes = sb.tile([P, S], U32, align_bytes=64)
+        z_scales = sb.tile([P, S], U8, align_bytes=64)
+        z_bf = [sb.tile([P, HALF, PACK], BF16, name="z_bf%d" % u, align_bytes=64) for u in range(2)]
+        for u in range(2):
+            nc.vector.scalar_tensor_tensor(
+                out=z_bf[u][:],
+                in0=h_banks[u][:].rearrange("p t j -> p j t"),
+                scalar=0.0625,
+                in1=gain[:, :, 0].unsqueeze(1).to_broadcast([P, HALF, PACK]),
+                op0=ALU.mult,
+                op1=ALU.mult,
+            )
+        for u in range(2):
+            cols = slice(u * HALF, (u + 1) * HALF)
+            nc.vector.quantize_mx(
+                out=z_codes[:, cols].bitcast(FP8X4),
+                scales=z_scales[:, cols],
+                in_=z_bf[u][:].rearrange("p j t -> p (j t)"),
+            )
+
+        ups, downs = [], []
+        for b in range(N // P):
+            cols = slice(b * P, (b + 1) * P)
+            bank = ps.tile([P, S], F32, name="h2_%d" % b)
+            nc.tensor.matmul_mx(
+                out=bank[:],
+                lhsT=w_codes[:, cols].bitcast(FP8X4),
+                lhsT_scale=w_scales[:, cols],
+                rhs=z_codes[:].bitcast(FP8X4),
+                rhs_scale=z_scales[:],
+                start=True,
+                stop=True,
+            )
+            nc.vector.tensor_copy(rows[b][:, :S], bank[:])
+            partner = sb.tile([P, S], F32, name="partner%d" % b)
+            nc.scalar.activation(partner[:], rows[b][:].indirect(n3_t[:]), COPY)
+            up = sb.tile([P, S], F32, name="up%d" % b)
+            down = sb.tile([P, S], F32, name="down%d" % b)
+            nc.vector.tensor_tensor(up[:], rows[b][:, :S], partner[:], ALU.max)
+            nc.vector.tensor_tensor(down[:], rows[b][:, :S], partner[:], ALU.min)
+            ups.append(up)
+            downs.append(down)
+
+        pages = [sb.tile([P, U], F32, name="page%d" % b) for b in range(N // P)]
+        for b in range(N // P):
+            nc.scalar.activation(pages[b][:].indirect(n1_t[:]), ups[b][:], COPY)
+        for b in range(N // P):
+            nc.scalar.activation(pages[b][:].indirect(n2_t[:]), downs[b][:], COPY)
+            nc.sync.dma_start(out[b * P : (b + 1) * P, :], pages[b][:])

@@ -1,4 +1,5 @@
 import concourse.mybir as mybir
+from concourse.masks import make_identity
 
 K, T, S, N, G, H, U = 512, 1024, 256, 512, 2048, 512, 512
 FLOPS = 2 * (2 * K * H * S + H * N * S)
@@ -37,15 +38,15 @@ def tile_picked_haqipagmx_none_p_kernel(
 
         d_bytes = sb.tile([P, G], U8, align_bytes=64)
         x_bytes = sb.tile([P, T], U8, align_bytes=64)
+        offs_t = load_list(offs, "offs_t")
+        nc.sync.dma_start(
+            x_bytes[:].bitcast(I32), x_scales[0].bitcast(I32).unsqueeze(1).to_broadcast([P // RUN, RUN, T // 4])
+        )
         ka_t = load_list(ka, "ka_t")
         nc.sync.dma_start(
             d_bytes[:].bitcast(I32), d_scales[0].bitcast(I32).unsqueeze(1).to_broadcast([P // RUN, RUN, G // 4])
         )
         kb_t = load_list(kb, "kb_t")
-        offs_t = load_list(offs, "offs_t")
-        nc.sync.dma_start(
-            x_bytes[:].bitcast(I32), x_scales[0].bitcast(I32).unsqueeze(1).to_broadcast([P // RUN, RUN, T // 4])
-        )
 
         x_table = sb.tile([P, T], U32, align_bytes=64)
         d_table = sb.tile([P, G], U32, align_bytes=64)
@@ -55,38 +56,44 @@ def tile_picked_haqipagmx_none_p_kernel(
         n1_t = load_list(n1, "n1_t")
         n2_t = load_list(n2, "n2_t")
 
-        gain = sb.tile([P, PACK, 8], F32)
-        with nc.allow_non_contiguous_dma(reason="one gain for each partition and byte of a word"):
-            gn_view = gn.rearrange("(q t r) o -> t q r o", t=PACK, r=RUN)
-            for t in range(PACK):
-                nc.sync.dma_start(gain[:, t, 0:1], gn_view[t])
+        w_raw = sb.tile([P, PACK, N], F32, align_bytes=64)
+        w_view = w1.rearrange("(q t r) n -> t q r n", t=PACK, r=RUN)
+        for t in range(PACK):
+            nc.sync.dma_start(w_raw[:, t, :], w_view[t])
+
+        gain_rows = sb.tile([P, P], F32)
+        nc.gpsimd.memset(gain_rows[:], 0.0)
+        nc.gpsimd.dma_start(
+            gain_rows[0:PACK, :].rearrange("t (q r) -> t q r", r=RUN),
+            gn.rearrange("(q t r) o -> t q (r o)", t=PACK, r=RUN),
+        )
+        identity = sb.tile([P, P], F32)
+        make_identity(nc, identity[:])
+        gain_bank = ps.tile([P, P], F32)
+        nc.tensor.transpose(gain_bank[:], gain_rows[:], identity[:])
+        factor = sb.tile([P, PACK], F32)
+        nc.scalar.activation(factor[:], gain_bank[:, 0:PACK], COPY, scale=0.0625)
 
         scales = sb.tile([P, 2 * H + S], U8, align_bytes=64)
         nc.vector.memset(scales[:].bitcast(I32), 0)
         rows = []
         for b in range(N // P):
             row = sb.tile([P, S + SPARE], F32, name="row%d" % b)
-            nc.gpsimd.memset(row[:, S:], 0.0)
+            nc.vector.memset(row[:, S:], 0.0)
             rows.append(row)
 
-        picked_bytes = sb.tile([P, 2 * H + S], U8, tag="staging", align_bytes=64)
+        picked_bytes = sb.tile([P, 2 * H + S], U8, align_bytes=64)
+        nc.vector.tensor_copy(picked_bytes[:, 2 * H :], x_bytes[:].indirect(offs_t[:]))
         nc.vector.tensor_copy(picked_bytes[:, 0:H], d_bytes[:].indirect(ka_t[:]))
         nc.vector.tensor_copy(picked_bytes[:, H : 2 * H], d_bytes[:].indirect(kb_t[:]))
-        nc.vector.tensor_copy(picked_bytes[:, 2 * H :], x_bytes[:].indirect(offs_t[:]))
         dealt_bytes = sb.tile([P, 2 * H + S], U8, align_bytes=64)
+        nc.vector.tensor_copy(dealt_bytes[:, 2 * H :].bitcast(I32), picked_bytes[:, 2 * H :].bitcast(I32))
         nc.vector.tensor_copy(
             dealt_bytes[:, : 2 * H].bitcast(I32).rearrange("p (l t q w) -> p l t q w", l=2, t=PACK, w=2),
             picked_bytes[:, : 2 * H].bitcast(I32).rearrange("p (l q t w) -> p l t q w", l=2, t=PACK, w=2),
         )
-        nc.vector.tensor_copy(dealt_bytes[:, 2 * H :].bitcast(I32), picked_bytes[:, 2 * H :].bitcast(I32))
         for c in range(4):
-            queue = nc.sync if c % 2 == 0 else nc.scalar
-            queue.dma_start(scales[c:P:32, :].bitcast(I32), dealt_bytes[RUN * c : P : 32, :].bitcast(I32))
-
-        w_raw = sb.tile([P, PACK, N], F32, tag="staging", align_bytes=64)
-        w_view = w1.rearrange("(q t r) n -> t q r n", t=PACK, r=RUN)
-        for t in range(PACK):
-            nc.sync.dma_start(w_raw[:, t, :], w_view[t])
+            nc.sync.dma_start(scales[c:P:32, :].bitcast(I32), dealt_bytes[RUN * c : P : 32, :].bitcast(I32))
 
         x_codes = sb.tile([P, S], U32, align_bytes=64)
         nc.vector.tensor_copy(x_codes[:], x_table[:].indirect(offs_t[:]))
@@ -120,7 +127,7 @@ def tile_picked_haqipagmx_none_p_kernel(
         w_scales = sb.tile([P, N], U8, align_bytes=64)
         for b in range(N // P):
             cols = slice(b * P, (b + 1) * P)
-            w_bf = sb.tile([P, P, PACK], BF16, name="w_bf%d" % b, align_bytes=64)
+            w_bf = sb.tile([P, P, PACK], BF16, name="w_bf%d" % b, tag="rounded%d" % b, align_bytes=64)
             nc.scalar.activation(
                 w_bf[:].rearrange("p (c i) t -> p c t i", i=4),
                 w_raw[:, :, cols].rearrange("p t (c i) -> p c t i", i=4),
@@ -134,15 +141,13 @@ def tile_picked_haqipagmx_none_p_kernel(
 
         z_codes = sb.tile([P, S], U32, align_bytes=64)
         z_scales = sb.tile([P, S], U8, align_bytes=64)
-        z_bf = [sb.tile([P, HALF, PACK], BF16, name="z_bf%d" % u, align_bytes=64) for u in range(2)]
+        z_bf = [sb.tile([P, HALF, PACK], BF16, name="z_bf%d" % u, tag="rounded%d" % u, align_bytes=64) for u in range(2)]
         for u in range(2):
-            nc.vector.scalar_tensor_tensor(
-                out=z_bf[u][:],
-                in0=h_banks[u][:].rearrange("p t j -> p j t"),
-                scalar=0.0625,
-                in1=gain[:, :, 0].unsqueeze(1).to_broadcast([P, HALF, PACK]),
-                op0=ALU.mult,
-                op1=ALU.mult,
+            nc.vector.tensor_tensor(
+                z_bf[u][:],
+                h_banks[u][:].rearrange("p t j -> p j t"),
+                factor[:].unsqueeze(1).to_broadcast([P, HALF, PACK]),
+                ALU.mult,
             )
         for u in range(2):
             cols = slice(u * HALF, (u + 1) * HALF)
@@ -152,12 +157,12 @@ def tile_picked_haqipagmx_none_p_kernel(
                 in_=z_bf[u][:].rearrange("p j t -> p (j t)"),
             )
 
-        ups, downs = [], []
-        for b in range(N // P):
+        blocks = range(N // P)
+        banks = [ps.tile([P, S], F32, name="h2_%d" % b) for b in blocks]
+        for b in blocks:
             cols = slice(b * P, (b + 1) * P)
-            bank = ps.tile([P, S], F32, name="h2_%d" % b)
             nc.tensor.matmul_mx(
-                out=bank[:],
+                out=banks[b][:],
                 lhsT=w_codes[:, cols].bitcast(FP8X4),
                 lhsT_scale=w_scales[:, cols],
                 rhs=z_codes[:].bitcast(FP8X4),
@@ -165,15 +170,16 @@ def tile_picked_haqipagmx_none_p_kernel(
                 start=True,
                 stop=True,
             )
-            nc.vector.tensor_copy(rows[b][:, :S], bank[:])
-            partner = sb.tile([P, S], F32, name="partner%d" % b)
-            nc.scalar.activation(partner[:], rows[b][:].indirect(n3_t[:]), COPY)
-            up = sb.tile([P, S], F32, name="up%d" % b)
-            down = sb.tile([P, S], F32, name="down%d" % b)
-            nc.vector.tensor_tensor(up[:], rows[b][:, :S], partner[:], ALU.max)
-            nc.vector.tensor_tensor(down[:], rows[b][:, :S], partner[:], ALU.min)
-            ups.append(up)
-            downs.append(down)
+            nc.vector.tensor_copy(rows[b][:, :S], banks[b][:])
+        partners = [sb.tile([P, S], F32, name="partner%d" % b) for b in blocks]
+        for b in blocks:
+            nc.scalar.activation(partners[b][:], rows[b][:].indirect(n3_t[:]), COPY)
+        ups = [sb.tile([P, S], F32, name="up%d" % b) for b in blocks]
+        downs = [sb.tile([P, S], F32, name="down%d" % b) for b in blocks]
+        for b in blocks:
+            nc.vector.tensor_tensor(ups[b][:], rows[b][:, :S], partners[b][:], ALU.max)
+        for b in blocks:
+            nc.vector.tensor_tensor(downs[b][:], rows[b][:, :S], partners[b][:], ALU.min)
 
         pages = [sb.tile([P, U], F32, name="page%d" % b) for b in range(N // P)]
         for b in range(N // P):

@@ -38,28 +38,31 @@ def tile_picked_haqipagmx_none_p_kernel(
 
         d_bytes = sb.tile([P, G], U8, align_bytes=64)
         x_bytes = sb.tile([P, T], U8, align_bytes=64)
-        offs_t = load_list(offs, "offs_t")
-        nc.sync.dma_start(
-            x_bytes[:].bitcast(I32), x_scales[0].bitcast(I32).unsqueeze(1).to_broadcast([P // RUN, RUN, T // 4])
-        )
+        nc.gpsimd.memset(d_bytes[:].bitcast(I32), 0)
+        nc.vector.memset(x_bytes[:].bitcast(I32), 0)
         ka_t = load_list(ka, "ka_t")
-        nc.sync.dma_start(
-            d_bytes[:].bitcast(I32), d_scales[0].bitcast(I32).unsqueeze(1).to_broadcast([P // RUN, RUN, G // 4])
-        )
         kb_t = load_list(kb, "kb_t")
+        offs_t = load_list(offs, "offs_t")
+        nc.sync.dma_start(d_bytes[0:P:RUN, :].bitcast(I32), d_scales[0].bitcast(I32))
+        nc.sync.dma_start(x_bytes[0:P:RUN, :].bitcast(I32), x_scales[0].bitcast(I32))
+        n3_t = load_list(n3, "n3_t")
+        n1_t = load_list(n1, "n1_t")
 
         x_table = sb.tile([P, T], U32, align_bytes=64)
         d_table = sb.tile([P, G], U32, align_bytes=64)
-        nc.sync.dma_start(x_table[:].bitcast(I32), x_words[0].rearrange("p c t -> p (c t)").bitcast(I32))
         nc.sync.dma_start(d_table[:].bitcast(I32), d_words[0].rearrange("p c t -> p (c t)").bitcast(I32))
-        n3_t = load_list(n3, "n3_t")
-        n1_t = load_list(n1, "n1_t")
+        nc.sync.dma_start(x_table[:].bitcast(I32), x_words[0].rearrange("p c t -> p (c t)").bitcast(I32))
         n2_t = load_list(n2, "n2_t")
 
-        w_raw = sb.tile([P, PACK, N], F32, align_bytes=64)
         w_view = w1.rearrange("(q t r) n -> t q r n", t=PACK, r=RUN)
-        for t in range(PACK):
-            nc.sync.dma_start(w_raw[:, t, :], w_view[t])
+
+        def load_weights(half, tag):
+            raw = sb.tile([P, PACK, N // 2], F32, name="w_raw%d" % half, tag=tag, align_bytes=64)
+            for t in range(PACK):
+                nc.sync.dma_start(raw[:, t, :], w_view[t][:, :, half * (N // 2) : (half + 1) * (N // 2)])
+            return raw
+
+        w_raw = [load_weights(0, "w_first")]
 
         gain_rows = sb.tile([P, P], F32)
         nc.gpsimd.memset(gain_rows[:], 0.0)
@@ -82,9 +85,9 @@ def tile_picked_haqipagmx_none_p_kernel(
             nc.vector.memset(row[:, S:], 0.0)
             rows.append(row)
 
-        picked_bytes = sb.tile([P, 2 * H + S], U8, align_bytes=64)
-        nc.vector.tensor_copy(picked_bytes[:, 2 * H :], x_bytes[:].indirect(offs_t[:]))
+        picked_bytes = sb.tile([P, 2 * H + S], U8, tag="staging", align_bytes=64)
         nc.vector.tensor_copy(picked_bytes[:, 0:H], d_bytes[:].indirect(ka_t[:]))
+        nc.vector.tensor_copy(picked_bytes[:, 2 * H :], x_bytes[:].indirect(offs_t[:]))
         nc.vector.tensor_copy(picked_bytes[:, H : 2 * H], d_bytes[:].indirect(kb_t[:]))
         dealt_bytes = sb.tile([P, 2 * H + S], U8, align_bytes=64)
         nc.vector.tensor_copy(dealt_bytes[:, 2 * H :].bitcast(I32), picked_bytes[:, 2 * H :].bitcast(I32))
@@ -95,12 +98,15 @@ def tile_picked_haqipagmx_none_p_kernel(
         for c in range(4):
             nc.sync.dma_start(scales[c:P:32, :].bitcast(I32), dealt_bytes[RUN * c : P : 32, :].bitcast(I32))
 
+        w_raw.append(load_weights(1, "staging"))
+
         x_codes = sb.tile([P, S], U32, align_bytes=64)
-        nc.vector.tensor_copy(x_codes[:], x_table[:].indirect(offs_t[:]))
         d_codes = []
         for name, index in (("a", ka_t), ("b", kb_t)):
             picked = sb.tile([P, H], U32, name="picked_" + name, align_bytes=64)
             nc.vector.tensor_copy(picked[:], d_table[:].indirect(index[:]))
+            if name == "a":
+                nc.vector.tensor_copy(x_codes[:], x_table[:].indirect(offs_t[:]))
             dealt = sb.tile([P, H], U32, name="dealt_" + name, align_bytes=64)
             nc.vector.tensor_copy(
                 dealt[:].bitcast(I32).rearrange("p (t q r) -> p t q r", t=PACK, r=RUN),
@@ -130,7 +136,7 @@ def tile_picked_haqipagmx_none_p_kernel(
             w_bf = sb.tile([P, P, PACK], BF16, name="w_bf%d" % b, tag="rounded%d" % b, align_bytes=64)
             nc.scalar.activation(
                 w_bf[:].rearrange("p (c i) t -> p c t i", i=4),
-                w_raw[:, :, cols].rearrange("p t (c i) -> p c t i", i=4),
+                w_raw[b // 2][:, :, (b % 2) * P : (b % 2 + 1) * P].rearrange("p t (c i) -> p c t i", i=4),
                 COPY,
             )
             nc.vector.quantize_mx(

@@ -135,8 +135,8 @@ def tile_picked_haqipagmx_none_p_kernel(
             cols = slice(b * P, (b + 1) * P)
             w_bf = sb.tile([P, P, PACK], BF16, name="w_bf%d" % b, tag="rounded%d" % b, align_bytes=64)
             nc.scalar.activation(
-                w_bf[:].rearrange("p (c i) t -> p c t i", i=4),
-                w_raw[b // 2][:, :, (b % 2) * P : (b % 2 + 1) * P].rearrange("p t (c i) -> p c t i", i=4),
+                w_bf[:],
+                w_raw[b // 2][:, :, (b % 2) * P : (b % 2 + 1) * P].rearrange("p t m -> p m t"),
                 COPY,
             )
             nc.vector.quantize_mx(
@@ -164,19 +164,22 @@ def tile_picked_haqipagmx_none_p_kernel(
             )
 
         blocks = range(N // P)
-        banks = [ps.tile([P, S], F32, name="h2_%d" % b) for b in blocks]
         for b in blocks:
             cols = slice(b * P, (b + 1) * P)
-            nc.tensor.matmul_mx(
-                out=banks[b][:],
-                lhsT=w_codes[:, cols].bitcast(FP8X4),
-                lhsT_scale=w_scales[:, cols],
-                rhs=z_codes[:].bitcast(FP8X4),
-                rhs_scale=z_scales[:],
-                start=True,
-                stop=True,
-            )
-            nc.vector.tensor_copy(rows[b][:, :S], banks[b][:])
+            width = HALF if b == 0 else S
+            for start in range(0, S, width):
+                places = slice(start, start + width)
+                bank = ps.tile([P, width], F32, name="h2_%d_%d" % (b, start))
+                nc.tensor.matmul_mx(
+                    out=bank[:],
+                    lhsT=w_codes[:, cols].bitcast(FP8X4),
+                    lhsT_scale=w_scales[:, cols],
+                    rhs=z_codes[:, places].bitcast(FP8X4),
+                    rhs_scale=z_scales[:, places],
+                    start=True,
+                    stop=True,
+                )
+                nc.vector.tensor_copy(rows[b][:, places], bank[:])
         partners = [sb.tile([P, S], F32, name="partner%d" % b) for b in blocks]
         for b in blocks:
             nc.scalar.activation(partners[b][:], rows[b][:].indirect(n3_t[:]), COPY)

import concourse.mybir as mybir
from concourse.masks import make_identity

K, T, S, N, G, H, U = 512, 1024, 256, 512, 2048, 512, 512
FLOPS = 2 * (2 * K * H * S + H * N * S)

F32 = mybir.dt.float32
BF16 = mybir.dt.bfloat16
I32 = mybir.dt.int32
U32 = mybir.dt.uint32
U16 = mybir.dt.uint16
U8 = mybir.dt.uint8
FP8X4 = mybir.dt.float8_e4m3fn_x4
ALU = mybir.AluOpType
COPY = mybir.ActivationFunctionType.Copy

P = 128
PACK = 4
RUN = 8
HALF = S // 2
SPARE = 16


def tile_picked_haqipagmx_none_p_kernel(
    tc, x_words, x_scales, d_words, d_scales, gn, w1, offs, ka, kb, n1, n2, n3, out
):
    nc = tc.nc
    with (
        tc.tile_pool(name="lists", bufs=1) as lists,
        tc.tile_pool(name="sb", bufs=1) as sb,
        tc.psum_pool(name="ps", bufs=1) as ps,
    ):

        def load_list(src, name):
            tile = lists.tile(list(src.shape), U16, name=name)
            nc.sync.dma_start(tile[:], src)
            return tile

        d_bytes = sb.tile([P, G], U8, align_bytes=64)
        x_bytes = sb.tile([P, T], U8, align_bytes=64)
        nc.gpsimd.memset(d_bytes[:].bitcast(I32), 0)
        nc.vector.memset(x_bytes[:].bitcast(I32), 0)
        ka_t = load_list(ka, "ka_t")
        kb_t = load_list(kb, "kb_t")
        offs_t = load_list(offs, "offs_t")
        nc.sync.dma_start(d_bytes[0:P:RUN, :].bitcast(I32), d_scales[0].bitcast(I32))
        nc.sync.dma_start(x_bytes[0:P:RUN, :].bitcast(I32), x_scales[0].bitcast(I32))
        n3_t = load_list(n3, "n3_t")
        n1_t = load_list(n1, "n1_t")

        x_table = sb.tile([P, T], U32, align_bytes=64)
        d_table = sb.tile([P, G], U32, align_bytes=64)
        nc.sync.dma_start(d_table[:].bitcast(I32), d_words[0].rearrange("p c t -> p (c t)").bitcast(I32))
        nc.sync.dma_start(x_table[:].bitcast(I32), x_words[0].rearrange("p c t -> p (c t)").bitcast(I32))
        n2_t = load_list(n2, "n2_t")

        w_view = w1.rearrange("(q t r) n -> t q r n", t=PACK, r=RUN)

        def load_weights(half, tag):
            raw = sb.tile([P, PACK, N // 2], F32, name="w_raw%d" % half, tag=tag, align_bytes=64)
            for t in range(PACK):
                nc.sync.dma_start(raw[:, t, :], w_view[t][:, :, half * (N // 2) : (half + 1) * (N // 2)])
            return raw

        w_raw = [load_weights(0, "w_first")]

        gain_rows = sb.tile([P, P], F32)
        nc.gpsimd.memset(gain_rows[:], 0.0)
        nc.gpsimd.dma_start(
            gain_rows[0:PACK, :].rearrange("t (q r) -> t q r", r=RUN),
            gn.rearrange("(q t r) o -> t q (r o)", t=PACK, r=RUN),
        )
        identity = sb.tile([P, P], F32)
        make_identity(nc, identity[:])
        gain_bank = ps.tile([P, P], F32)
        nc.tensor.transpose(gain_bank[:], gain_rows[:], identity[:])
        factor = sb.tile([P, PACK], F32)
        nc.scalar.activation(factor[:], gain_bank[:, 0:PACK], COPY, scale=0.0625)

        scales = sb.tile([P, 2 * H + S], U8, align_bytes=64)
        nc.vector.memset(scales[:].bitcast(I32), 0)
        rows = []
        for b in range(N // P):
            row = sb.tile([P, S + SPARE], F32, name="row%d" % b)
            nc.vector.memset(row[:, S:], 0.0)
            rows.append(row)

        picked_bytes = sb.tile([P, 2 * H + S], U8, tag="staging", align_bytes=64)
        nc.vector.tensor_copy(picked_bytes[:, 0:H], d_bytes[:].indirect(ka_t[:]))
        nc.vector.tensor_copy(picked_bytes[:, 2 * H :], x_bytes[:].indirect(offs_t[:]))
        nc.vector.tensor_copy(picked_bytes[:, H : 2 * H], d_bytes[:].indirect(kb_t[:]))
        dealt_bytes = sb.tile([P, 2 * H + S], U8, align_bytes=64)
        nc.vector.tensor_copy(dealt_bytes[:, 2 * H :].bitcast(I32), picked_bytes[:, 2 * H :].bitcast(I32))
        nc.vector.tensor_copy(
            dealt_bytes[:, : 2 * H].bitcast(I32).rearrange("p (l t q w) -> p l t q w", l=2, t=PACK, w=2),
            picked_bytes[:, : 2 * H].bitcast(I32).rearrange("p (l q t w) -> p l t q w", l=2, t=PACK, w=2),
        )
        for c in range(4):
            nc.sync.dma_start(scales[c:P:32, :].bitcast(I32), dealt_bytes[RUN * c : P : 32, :].bitcast(I32))

        w_raw.append(load_weights(1, "staging"))

        x_codes = sb.tile([P, S], U32, align_bytes=64)
        d_codes = []
        for name, index in (("a", ka_t), ("b", kb_t)):
            picked = sb.tile([P, H], U32, name="picked_" + name, align_bytes=64)
            nc.vector.tensor_copy(picked[:], d_table[:].indirect(index[:]))
            if name == "a":
                nc.vector.tensor_copy(x_codes[:], x_table[:].indirect(offs_t[:]))
            dealt = sb.tile([P, H], U32, name="dealt_" + name, align_bytes=64)
            nc.vector.tensor_copy(
                dealt[:].bitcast(I32).rearrange("p (t q r) -> p t q r", t=PACK, r=RUN),
                picked[:].bitcast(I32).rearrange("p (q t r) -> p t q r", t=PACK, r=RUN),
            )
            d_codes.append(dealt)

        h_banks = [ps.tile([P, PACK, HALF], F32, name="h%d" % u) for u in range(2)]
        for l in range(2):
            for u in range(2):
                cols = slice(u * HALF, (u + 1) * HALF)
                for t in range(PACK):
                    nc.tensor.matmul_mx(
                        out=h_banks[u][:, t, :],
                        lhsT=d_codes[l][:, t * P : (t + 1) * P].bitcast(FP8X4),
                        lhsT_scale=scales[:, l * H + t * P : l * H + (t + 1) * P],
                        rhs=x_codes[:, cols].bitcast(FP8X4),
                        rhs_scale=scales[:, 2 * H + u * HALF : 2 * H + (u + 1) * HALF],
                        start=(l == 0 and t == 0),
                        stop=(l == 1 and t == PACK - 1),
                    )

        w_codes = sb.tile([P, N], U32, align_bytes=64)
        w_scales = sb.tile([P, N], U8, align_bytes=64)
        for b in range(N // P):
            cols = slice(b * P, (b + 1) * P)
            w_bf = sb.tile([P, P, PACK], BF16, name="w_bf%d" % b, tag="rounded%d" % b, align_bytes=64)
            nc.scalar.activation(
                w_bf[:],
                w_raw[b // 2][:, :, (b % 2) * P : (b % 2 + 1) * P].rearrange("p t m -> p m t"),
                COPY,
            )
            nc.vector.quantize_mx(
                out=w_codes[:, cols].bitcast(FP8X4),
                scales=w_scales[:, cols],
                in_=w_bf[:].rearrange("p m t -> p (m t)"),
            )

        z_codes = sb.tile([P, S], U32, align_bytes=64)
        z_scales = sb.tile([P, S], U8, align_bytes=64)
        z_bf = [sb.tile([P, HALF, PACK], BF16, name="z_bf%d" % u, tag="rounded%d" % u, align_bytes=64) for u in range(2)]
        for u in range(2):
            nc.vector.tensor_tensor(
                z_bf[u][:],
                h_banks[u][:].rearrange("p t j -> p j t"),
                factor[:].unsqueeze(1).to_broadcast([P, HALF, PACK]),
                ALU.mult,
            )
        for u in range(2):
            cols = slice(u * HALF, (u + 1) * HALF)
            nc.vector.quantize_mx(
                out=z_codes[:, cols].bitcast(FP8X4),
                scales=z_scales[:, cols],
                in_=z_bf[u][:].rearrange("p j t -> p (j t)"),
            )

        blocks = range(N // P)
        for b in blocks:
            cols = slice(b * P, (b + 1) * P)
            width = HALF if b == 0 else S
            for start in range(0, S, width):
                places = slice(start, start + width)
                bank = ps.tile([P, width], F32, name="h2_%d_%d" % (b, start))
                nc.tensor.matmul_mx(
                    out=bank[:],
                    lhsT=w_codes[:, cols].bitcast(FP8X4),
                    lhsT_scale=w_scales[:, cols],
                    rhs=z_codes[:, places].bitcast(FP8X4),
                    rhs_scale=z_scales[:, places],
                    start=True,
                    stop=True,
                )
                nc.vector.tensor_copy(rows[b][:, places], bank[:])
        partners = [sb.tile([P, S], F32, name="partner%d" % b) for b in blocks]
        for b in blocks:
            nc.scalar.activation(partners[b][:], rows[b][:].indirect(n3_t[:]), COPY)
        ups = [sb.tile([P, S], F32, name="up%d" % b) for b in blocks]
        downs = [sb.tile([P, S], F32, name="down%d" % b) for b in blocks]
        for b in blocks:
            nc.vector.tensor_tensor(ups[b][:], rows[b][:, :S], partners[b][:], ALU.max)
        for b in blocks:
            nc.vector.tensor_tensor(downs[b][:], rows[b][:, :S], partners[b][:], ALU.min)

        pages = [sb.tile([P, U], F32, name="page%d" % b) for b in range(N // P)]
        for b in range(N // P):
            nc.scalar.activation(pages[b][:].indirect(n1_t[:]), ups[b][:], COPY)
        for b in range(N // P):
            nc.scalar.activation(pages[b][:].indirect(n2_t[:]), downs[b][:], COPY)
            nc.sync.dma_start(out[b * P : (b + 1) * P, :], pages[b][:])
